import numpy as np
import ml_dtypes


def mxq(x, axis, fmt="e4m3"):
    dtype, down = {"e4m3": (ml_dtypes.float8_e4m3fn, 7), "e5m2": (ml_dtypes.float8_e5m2, 14)}[fmt]
    v = np.moveaxis(np.asarray(x, np.float32).astype(ml_dtypes.bfloat16).astype(np.float64), axis, -1)
    blocks = v.reshape(v.shape[:-1] + (-1, 32))
    amax = np.abs(blocks).max(-1, keepdims=True)
    byte = np.maximum(np.where(amax > 0, np.frexp(amax)[1] - 1 + 127, 0) - down, 1)
    scale = np.exp2(byte - 127.0)
    codes = (blocks / scale).astype(np.float32).astype(dtype).astype(np.float64)
    return np.moveaxis((codes * scale).reshape(v.shape), -1, axis)


WIDE = False


def mx_kscale(k):
    if not WIDE:
        return np.ones(k)
    levels = np.array([10, -10, 5, -5, 0])
    if k % 512:
        return np.exp2(np.random.permutation(np.resize(levels, k // 32))).repeat(32)
    a = np.empty((k // 512, 16))
    for p in range(k // 512):
        a[p, :8] = np.random.permutation(np.resize(levels, 8))
        for g in range(8):
            far = levels[np.abs(levels - a[p, g]) >= 10]
            a[p, g + 8] = far[np.random.randint(len(far))]
    return np.exp2(a.ravel()).repeat(32)


def f64(x):
    return np.asarray(x).astype(np.float64)


def striped(idx):
    return np.tile(idx.reshape(-1, 16).T, (8, 1)).astype(np.uint16)


def unstriped(offs):
    return offs[:16].T.reshape(-1).astype(np.int64)


def pack_weight(w):
    k, n = w.shape
    w = f64(np.asarray(w, np.float32).astype(ml_dtypes.bfloat16)).reshape(k // 32, 32, n)
    amax = np.abs(w).max(1)
    byte = np.clip(np.where(amax > 0, np.frexp(amax)[1] - 1 + 127 - 7, 1), 1, 254)
    scaled = (w * np.exp2(127.0 - byte)[:, None, :]).reshape(k, n).astype(np.float32)
    words = np.ascontiguousarray(scaled.reshape(k // 512, 128, 4, n).transpose(0, 1, 3, 2)).astype(ml_dtypes.float8_e4m3fn).view(np.uint8)
    return words, np.ascontiguousarray(byte.astype(np.uint8).reshape(k // 512, 16, n))


def unpack_weight(words, scales):
    g, p, n, _ = words.shape
    vals = np.ascontiguousarray(words).view(ml_dtypes.float8_e4m3fn).astype(np.float64) * np.repeat(np.exp2(scales.astype(np.float64) - 127.0), 8, axis=1)[..., None]
    return vals.transpose(0, 1, 3, 2).reshape(g * 512, n)


K, T, E, C, N = 2048, 1024, 4, 256, 128


def by_expert(wq, xq):
    return np.concatenate([wq[e].T @ xq[:, e * C:(e + 1) * C] for e in range(E)], axis=1)


def setup_inputs():
    n = np.random.standard_normal
    s = mx_kscale(K)[:, None]
    packed = [pack_weight(m) for m in n((E, K, N)) / np.sqrt(K) / s[None]]
    return {
        "xT": (n((K, T)) * s).astype(np.float32),
        "w_words": np.stack([m[0] for m in packed]),
        "w_scales": np.stack([m[1] for m in packed]),
        "gate": np.tile(np.random.uniform(0.2, 1.0, E * C), (N, 1)).astype(np.float32),
        "offs": striped(np.random.permutation(T)[:E * C]),
    }


def reference(xT, w_words, w_scales, gate, offs):
    idx = unstriped(offs)
    xq = mxq(f64(xT)[:, idx], 0, "e4m3")
    w = np.stack([unpack_weight(w_words[e], w_scales[e]) for e in range(E)])
    y = by_expert(w, xq)
    out = np.zeros((N, T))
    out[:, idx] = f64(gate) * y
    return out

@@ -1,0 +1,136 @@
+from contextlib import ExitStack
+
+import concourse.mybir as mybir
+
+F32 = mybir.dt.float32
+BF16 = mybir.dt.bfloat16
+U32 = mybir.dt.uint32
+I32 = mybir.dt.int32
+U16 = mybir.dt.uint16
+U8 = mybir.dt.uint8
+FP8X4 = mybir.dt.float8_e4m3fn_x4
+MULT = mybir.AluOpType.mult
+ADD = mybir.AluOpType.add
+
+K, T, E, C, N = 2048, 1024, 4, 256, 128
+P = 128
+PASSES = K // 512
+HALF = 512
+HALVES = E * C // HALF
+LIST_COLS = HALF // 16
+
+FLOPS = 2 * K * N * E * C
+
+VECTOR_CAST = {0: 448}
+GPSIMD_CAST = 480
+VECTOR_INTERLEAVE = ()
+
+
+def tile_routed_moe_kernel(tc, xT, w_words, w_scales, gate, offs, out):
+    nc = tc.nc
+    with ExitStack() as ctx:
+        lists = ctx.enter_context(tc.tile_pool(name="lists", bufs=1))
+        keep = ctx.enter_context(tc.tile_pool(name="keep", bufs=1))
+        psum = ctx.enter_context(tc.psum_pool(name="psum", bufs=1))
+
+        offsets = lists.tile([P, E * C // 16], U16, name="offsets")
+
+        x_view = xT.rearrange("(g p u j) n -> g u p j n", p=P, u=2, j=2)
+        raw = {}
+        for g in range(PASSES):
+            for u in range(2):
+                raw[g, u] = keep.tile([P, 2, T], F32, name="raw%d%d" % (g, u))
+                nc.sync.dma_start(raw[g, u][:], x_view[g, u])
+                if (g, u) == (0, 0):
+                    nc.sync.dma_start(offsets[:], offs)
+
+        w_codes = keep.tile([P, E * PASSES, N], I32, name="w_codes", align_bytes=64)
+        nc.sync.dma_start(w_codes[:], w_words.bitcast(I32).rearrange("e a p n o -> p (e a) (n o)"))
+
+        w_planes = keep.tile([P, E * PASSES, N], U8, name="w_planes", align_bytes=64)
+        nc.vector.memset(w_planes[:].rearrange("p s n -> p (s n)").bitcast(I32), 0)
+        planes_i32 = w_planes[:].bitcast(I32)
+        scales_i32 = w_scales.bitcast(I32).rearrange("e a (q r) n -> r q (e a) n", r=4)
+        for r in range(4):
+            nc.sync.dma_start(planes_i32[r:P:32, :, :], scales_i32[r])
+
+        gate_sb = keep.tile([P, E * C], F32, name="gate_sb")
+        nc.sync.dma_start(gate_sb[:], gate)
+
+        acc = [psum.tile([P, C], F32, name="acc%d" % e) for e in range(E)]
+        sums = [keep.tile([P, HALF], F32, name="sums%d" % h) for h in range(HALVES)]
+        result = keep.tile([P, T], F32, name="result")
+
+        def cast(g, u):
+            pairs = keep.tile([P, 2 * T], BF16, name="pairs%d%d" % (g, u))
+            dst = pairs[:].rearrange("p (n j) -> p n j", j=2)
+            src = raw[g, u][:].rearrange("p j n -> p n j")
+            cut = VECTOR_CAST.get(2 * g + u, 0)
+            if cut:
+                nc.vector.tensor_copy(out=dst[:, 0:cut, :], in_=src[:, 0:cut, :])
+            mid = cut + GPSIMD_CAST
+            nc.gpsimd.tensor_scalar(
+                out=dst[:, cut:mid, :], in0=src[:, cut:mid, :], scalar1=1.0, scalar2=0.0, op0=MULT, op1=ADD
+            )
+            nc.scalar.copy(out=dst[:, mid:T, :], in_=src[:, mid:T, :])
+            return pairs
+
+        def gather(pairs, rows, u, h):
+            window = pairs[:].bitcast(U32)
+            nc.vector.tensor_copy(rows[:, u, :], window.indirect(offsets[:, h * LIST_COLS : (h + 1) * LIST_COLS]))
+
+        def interleave(rows, g, h):
+            grouped = keep.tile([P, 4 * HALF], BF16, name="grouped%d%d" % (g, h), align_bytes=64)
+            if (g, h) in VECTOR_INTERLEAVE:
+                nc.vector.tensor_copy(
+                    out=grouped[:].bitcast(I32).rearrange("p (c u) -> p c u", u=2),
+                    in_=rows[:].bitcast(I32).rearrange("p u c -> p c u"),
+                )
+            else:
+                nc.scalar.copy(
+                    out=grouped[:].bitcast(U32).rearrange("p (c u) -> p c u", u=2),
+                    in_=rows[:].rearrange("p u c -> p c u"),
+                )
+            return grouped
+
+        def quantize(grouped, g, h):
+            codes = keep.tile([P, HALF], U32, name="codes%d%d" % (g, h), align_bytes=64)
+            planes = keep.tile([P, HALF], U8, name="planes%d%d" % (g, h), align_bytes=64)
+            nc.vector.quantize_mx(out=codes[:].bitcast(FP8X4), scales=planes[:], in_=grouped[:])
+            return codes, planes
+
+        def multiply(codes, planes, g, h):
+            for i in range(HALF // C):
+                e = h * (HALF // C) + i
+                cols = slice(i * C, (i + 1) * C)
+                nc.tensor.matmul_mx(
+                    out=acc[e][:],
+                    lhsT=w_codes[:, e * PASSES + g, :].bitcast(FP8X4),
+                    lhsT_scale=w_planes[:, e * PASSES + g, :],
+                    rhs=codes[:, cols].bitcast(FP8X4),
+                    rhs_scale=planes[:, cols],
+                    start=(g == 0),
+                    stop=(g == PASSES - 1),
+                )
+
+        for g in range(PASSES):
+            pairs = [cast(g, u) for u in range(2)]
+            rows = [keep.tile([P, 2, HALF], U32, name="rows%d%d" % (g, h)) for h in range(HALVES)]
+            for u in range(2):
+                for h in range(HALVES):
+                    gather(pairs[u], rows[h], u, h)
+            for h in range(HALVES):
+                grouped = interleave(rows[h], g, h)
+                codes, planes = quantize(grouped, g, h)
+                multiply(codes, planes, g, h)
+
+        for h in range(HALVES):
+            for i in range(HALF // C):
+                nc.scalar.copy(out=sums[h][:, i * C : (i + 1) * C], in_=acc[h * (HALF // C) + i][:])
+            nc.vector.tensor_tensor(
+                out=result[:].indirect(offsets[:, h * LIST_COLS : (h + 1) * LIST_COLS]),
+                in0=sums[h][:],
+                in1=gate_sb[:, h * HALF : (h + 1) * HALF],
+                op=MULT,
+            )
+        nc.sync.dma_start(out, result[:])

@@ -24,6 +24,7 @@ FLOPS = 2 * K * N * E * C
 VECTOR_CAST = {0: 448}
 GPSIMD_CAST = 480
 VECTOR_INTERLEAVE = ()
+WIDE_PASSES = (0, 1, 2)
 
 
 def tile_routed_moe_kernel(tc, xT, w_words, w_scales, gate, offs, out):
@@ -79,30 +80,23 @@ def tile_routed_moe_kernel(tc, xT, w_words, w_scales, gate, offs, out):
             window = pairs[:].bitcast(U32)
             nc.vector.tensor_copy(rows[:, u, :], window.indirect(offsets[:, h * LIST_COLS : (h + 1) * LIST_COLS]))
 
-        def interleave(rows, g, h):
-            grouped = keep.tile([P, 4 * HALF], BF16, name="grouped%d%d" % (g, h), align_bytes=64)
-            if (g, h) in VECTOR_INTERLEAVE:
-                nc.vector.tensor_copy(
-                    out=grouped[:].bitcast(I32).rearrange("p (c u) -> p c u", u=2),
-                    in_=rows[:].bitcast(I32).rearrange("p u c -> p c u"),
-                )
-            else:
-                nc.scalar.copy(
-                    out=grouped[:].bitcast(U32).rearrange("p (c u) -> p c u", u=2),
-                    in_=rows[:].rearrange("p u c -> p c u"),
-                )
-            return grouped
+        def interleave(rows, grouped, h):
+            nc.scalar.copy(
+                out=grouped[:, 4 * HALF * h : 4 * HALF * (h + 1)].bitcast(U32).rearrange("p (c u) -> p c u", u=2),
+                in_=rows[:].rearrange("p u c -> p c u"),
+            )
 
-        def quantize(grouped, g, h):
-            codes = keep.tile([P, HALF], U32, name="codes%d%d" % (g, h), align_bytes=64)
-            planes = keep.tile([P, HALF], U8, name="planes%d%d" % (g, h), align_bytes=64)
-            nc.vector.quantize_mx(out=codes[:].bitcast(FP8X4), scales=planes[:], in_=grouped[:])
-            return codes, planes
+        def quantize(grouped, codes, planes, first, slots):
+            nc.vector.quantize_mx(
+                out=codes[:, first : first + slots].bitcast(FP8X4),
+                scales=planes[:, first : first + slots],
+                in_=grouped[:, 4 * first : 4 * (first + slots)],
+            )
 
         def multiply(codes, planes, g, h):
             for i in range(HALF // C):
                 e = h * (HALF // C) + i
-                cols = slice(i * C, (i + 1) * C)
+                cols = slice(e * C, (e + 1) * C)
                 nc.tensor.matmul_mx(
                     out=acc[e][:],
                     lhsT=w_codes[:, e * PASSES + g, :].bitcast(FP8X4),
@@ -119,10 +113,20 @@ def tile_routed_moe_kernel(tc, xT, w_words, w_scales, gate, offs, out):
             for u in range(2):
                 for h in range(HALVES):
                     gather(pairs[u], rows[h], u, h)
-            for h in range(HALVES):
-                grouped = interleave(rows[h], g, h)
-                codes, planes = quantize(grouped, g, h)
-                multiply(codes, planes, g, h)
+            grouped = keep.tile([P, 4 * E * C], BF16, name="grouped%d" % g, align_bytes=64)
+            codes = keep.tile([P, E * C], U32, name="codes%d" % g, align_bytes=64)
+            planes = keep.tile([P, E * C], U8, name="planes%d" % g, align_bytes=64)
+            if g in WIDE_PASSES:
+                for h in range(HALVES):
+                    interleave(rows[h], grouped, h)
+                quantize(grouped, codes, planes, 0, E * C)
+                for h in range(HALVES):
+                    multiply(codes, planes, g, h)
+            else:
+                for h in range(HALVES):
+                    interleave(rows[h], grouped, h)
+                    quantize(grouped, codes, planes, h * HALF, HALF)
+                    multiply(codes, planes, g, h)
 
         for h in range(HALVES):
             for i in range(HALF // C):

@@ -21,10 +21,12 @@ LIST_COLS = HALF // 16
 
 FLOPS = 2 * K * N * E * C
 
-VECTOR_CAST = {0: 448}
-GPSIMD_CAST = 480
-VECTOR_INTERLEAVE = ()
-WIDE_PASSES = (0, 1, 2)
+EARLY = {
+    0: ((0, 256, 128, 512), (512, 272, 96, 1024)),
+    1: ((0, 0, 240, 512), (512, 0, 240, 1024)),
+}
+LATER = ((0, 0, 480, 1024),)
+QUANTISERS = ((0, 0, 1024), (1, 0, 1024), (2, 0, 512), (3, 0, 512), (2, 512, 512), (3, 512, 512))
 
 
 def tile_routed_moe_kernel(tc, xT, w_words, w_scales, gate, offs, out):
@@ -40,8 +42,9 @@ def tile_routed_moe_kernel(tc, xT, w_words, w_scales, gate, offs, out):
         raw = {}
         for g in range(PASSES):
             for u in range(2):
-                raw[g, u] = keep.tile([P, 2, T], F32, name="raw%d%d" % (g, u))
-                nc.sync.dma_start(raw[g, u][:], x_view[g, u])
+                for part, (first, on_vector, on_gpsimd, last) in enumerate(EARLY.get(2 * g + u, LATER)):
+                    raw[g, u, part] = keep.tile([P, 2, last - first], F32, name="raw%d%d%d" % (g, u, part))
+                    nc.sync.dma_start(raw[g, u, part][:], x_view[g, u][:, :, first:last])
                 if (g, u) == (0, 0):
                     nc.sync.dma_start(offsets[:], offs)
 
@@ -63,17 +66,19 @@ def tile_routed_moe_kernel(tc, xT, w_words, w_scales, gate, offs, out):
         result = keep.tile([P, T], F32, name="result")
 
         def cast(g, u):
-            pairs = keep.tile([P, 2 * T], BF16, name="pairs%d%d" % (g, u))
+            last_pair = (g, u) == (PASSES - 1, 1)
+            pairs = keep.tile([P, 2 * T], BF16, name="pairs%d%d" % (g, u), tag="late" if last_pair else "pairs%d%d" % (g, u), align_bytes=64)
             dst = pairs[:].rearrange("p (n j) -> p n j", j=2)
-            src = raw[g, u][:].rearrange("p j n -> p n j")
-            cut = VECTOR_CAST.get(2 * g + u, 0)
-            if cut:
-                nc.vector.tensor_copy(out=dst[:, 0:cut, :], in_=src[:, 0:cut, :])
-            mid = cut + GPSIMD_CAST
-            nc.gpsimd.tensor_scalar(
-                out=dst[:, cut:mid, :], in0=src[:, cut:mid, :], scalar1=1.0, scalar2=0.0, op0=MULT, op1=ADD
-            )
-            nc.scalar.copy(out=dst[:, mid:T, :], in_=src[:, mid:T, :])
+            for part, (first, on_vector, on_gpsimd, last) in enumerate(EARLY.get(2 * g + u, LATER)):
+                src = raw[g, u, part][:].rearrange("p j n -> p n j")
+                cut = on_vector
+                mid = on_vector + on_gpsimd
+                if cut:
+                    nc.vector.tensor_copy(out=dst[:, first : first + cut, :], in_=src[:, 0:cut, :])
+                nc.gpsimd.tensor_scalar(
+                    out=dst[:, first + cut : first + mid, :], in0=src[:, cut:mid, :], scalar1=1.0, scalar2=0.0, op0=MULT, op1=ADD
+                )
+                nc.scalar.copy(out=dst[:, first + mid : last, :], in_=src[:, mid : last - first, :])
             return pairs
 
         def gather(pairs, rows, u, h):
@@ -93,40 +98,35 @@ def tile_routed_moe_kernel(tc, xT, w_words, w_scales, gate, offs, out):
                 in_=grouped[:, 4 * first : 4 * (first + slots)],
             )
 
-        def multiply(codes, planes, g, h):
-            for i in range(HALF // C):
-                e = h * (HALF // C) + i
-                cols = slice(e * C, (e + 1) * C)
-                nc.tensor.matmul_mx(
-                    out=acc[e][:],
-                    lhsT=w_codes[:, e * PASSES + g, :].bitcast(FP8X4),
-                    lhsT_scale=w_planes[:, e * PASSES + g, :],
-                    rhs=codes[:, cols].bitcast(FP8X4),
-                    rhs_scale=planes[:, cols],
-                    start=(g == 0),
-                    stop=(g == PASSES - 1),
-                )
+        def multiply(codes, planes, g, e):
+            cols = slice(e * C, (e + 1) * C)
+            nc.tensor.matmul_mx(
+                out=acc[e][:],
+                lhsT=w_codes[:, e * PASSES + g, :].bitcast(FP8X4),
+                lhsT_scale=w_planes[:, e * PASSES + g, :],
+                rhs=codes[:, cols].bitcast(FP8X4),
+                rhs_scale=planes[:, cols],
+                start=(g == 0),
+                stop=(g == PASSES - 1),
+            )
 
+        grouped = []
         for g in range(PASSES):
             pairs = [cast(g, u) for u in range(2)]
             rows = [keep.tile([P, 2, HALF], U32, name="rows%d%d" % (g, h)) for h in range(HALVES)]
             for u in range(2):
                 for h in range(HALVES):
                     gather(pairs[u], rows[h], u, h)
-            grouped = keep.tile([P, 4 * E * C], BF16, name="grouped%d" % g, align_bytes=64)
-            codes = keep.tile([P, E * C], U32, name="codes%d" % g, align_bytes=64)
-            planes = keep.tile([P, E * C], U8, name="planes%d" % g, align_bytes=64)
-            if g in WIDE_PASSES:
-                for h in range(HALVES):
-                    interleave(rows[h], grouped, h)
-                quantize(grouped, codes, planes, 0, E * C)
-                for h in range(HALVES):
-                    multiply(codes, planes, g, h)
-            else:
-                for h in range(HALVES):
-                    interleave(rows[h], grouped, h)
-                    quantize(grouped, codes, planes, h * HALF, HALF)
-                    multiply(codes, planes, g, h)
+            grouped.append(keep.tile([P, 4 * E * C], BF16, name="grouped%d" % g, align_bytes=64))
+            for h in range(HALVES):
+                interleave(rows[h], grouped[g], h)
+
+        codes = keep.tile([P, PASSES, E * C], U32, name="codes", tag="late", align_bytes=64)
+        planes = keep.tile([P, PASSES, E * C], U8, name="planes", align_bytes=64)
+        for g, first, slots in QUANTISERS:
+            quantize(grouped[g], codes[:, g, :], planes[:, g, :], first, slots)
+            for e in range(first // C, (first + slots) // C):
+                multiply(codes[:, g, :], planes[:, g, :], g, e)
 
         for h in range(HALVES):
             for i in range(HALF // C):

@@ -21,12 +21,18 @@ LIST_COLS = HALF // 16
 
 FLOPS = 2 * K * N * E * C
 
-EARLY = {
-    0: ((0, 256, 128, 512), (512, 272, 96, 1024)),
+SHARES = {
+    0: ((0, 384, 176, 768), (768, 256, 0, 1024)),
     1: ((0, 0, 240, 512), (512, 0, 240, 1024)),
+    2: ((0, 0, 480, 1024),),
+    3: ((0, 0, 544, 1024),),
 }
-LATER = ((0, 0, 480, 1024),)
-QUANTISERS = ((0, 0, 1024), (1, 0, 1024), (2, 0, 512), (3, 0, 512), (2, 512, 512), (3, 512, 512))
+LATER = ((0, 0, 640, 1024),)
+LENDERS = {(1, 1): "grouped00", (2, 0): "grouped01", (2, 1): "grouped10", (3, 0): "grouped11", (3, 1): "grouped2"}
+GROUPED = {
+    (0, 0): ("grouped00", 1, 0), (0, 1): ("grouped01", 1, 0), (1, 0): ("grouped10", 1, 0), (1, 1): ("grouped11", 1, 0),
+    (2, 0): ("grouped2", 2, 0), (2, 1): ("grouped2", 2, 1), (3, 0): ("grouped3", 2, 0), (3, 1): ("grouped3", 2, 1),
+}
 
 
 def tile_routed_moe_kernel(tc, xT, w_words, w_scales, gate, offs, out):
@@ -42,11 +48,12 @@ def tile_routed_moe_kernel(tc, xT, w_words, w_scales, gate, offs, out):
         raw = {}
         for g in range(PASSES):
             for u in range(2):
-                for part, (first, on_vector, on_gpsimd, last) in enumerate(EARLY.get(2 * g + u, LATER)):
-                    raw[g, u, part] = keep.tile([P, 2, last - first], F32, name="raw%d%d%d" % (g, u, part))
+                for part, (first, on_vector, on_gpsimd, last) in enumerate(SHARES.get(2 * g + u, LATER)):
+                    name = "raw%d%d%d" % (g, u, part)
+                    raw[g, u, part] = keep.tile([P, 2, last - first], F32, name=name, tag=LENDERS.get((g, u), name), align_bytes=64)
                     nc.sync.dma_start(raw[g, u, part][:], x_view[g, u][:, :, first:last])
-                if (g, u) == (0, 0):
-                    nc.sync.dma_start(offsets[:], offs)
+                    if (g, u, part) == (0, 0, 0):
+                        nc.sync.dma_start(offsets[:], offs)
 
         w_codes = keep.tile([P, E * PASSES, N], I32, name="w_codes", align_bytes=64)
         nc.sync.dma_start(w_codes[:], w_words.bitcast(I32).rearrange("e a p n o -> p (e a) (n o)"))
@@ -69,34 +76,32 @@ def tile_routed_moe_kernel(tc, xT, w_words, w_scales, gate, offs, out):
             last_pair = (g, u) == (PASSES - 1, 1)
             pairs = keep.tile([P, 2 * T], BF16, name="pairs%d%d" % (g, u), tag="late" if last_pair else "pairs%d%d" % (g, u), align_bytes=64)
             dst = pairs[:].rearrange("p (n j) -> p n j", j=2)
-            for part, (first, on_vector, on_gpsimd, last) in enumerate(EARLY.get(2 * g + u, LATER)):
+            for part, (first, on_vector, on_gpsimd, last) in enumerate(SHARES.get(2 * g + u, LATER)):
                 src = raw[g, u, part][:].rearrange("p j n -> p n j")
                 cut = on_vector
                 mid = on_vector + on_gpsimd
                 if cut:
                     nc.vector.tensor_copy(out=dst[:, first : first + cut, :], in_=src[:, 0:cut, :])
-                nc.gpsimd.tensor_scalar(
-                    out=dst[:, first + cut : first + mid, :], in0=src[:, cut:mid, :], scalar1=1.0, scalar2=0.0, op0=MULT, op1=ADD
-                )
-                nc.scalar.copy(out=dst[:, first + mid : last, :], in_=src[:, mid : last - first, :])
+                if on_gpsimd:
+                    nc.gpsimd.tensor_scalar(
+                        out=dst[:, first + cut : first + mid, :], in0=src[:, cut:mid, :], scalar1=1.0, scalar2=0.0, op0=MULT, op1=ADD
+                    )
+                if first + mid < last:
+                    nc.scalar.copy(out=dst[:, first + mid : last, :], in_=src[:, mid : last - first, :])
             return pairs
 
         def gather(pairs, rows, u, h):
             window = pairs[:].bitcast(U32)
             nc.vector.tensor_copy(rows[:, u, :], window.indirect(offsets[:, h * LIST_COLS : (h + 1) * LIST_COLS]))
 
-        def interleave(rows, grouped, h):
+        def interleave(rows, grouped):
             nc.scalar.copy(
-                out=grouped[:, 4 * HALF * h : 4 * HALF * (h + 1)].bitcast(U32).rearrange("p (c u) -> p c u", u=2),
+                out=grouped.bitcast(U32).rearrange("p (c u) -> p c u", u=2),
                 in_=rows[:].rearrange("p u c -> p c u"),
             )
 
-        def quantize(grouped, codes, planes, first, slots):
-            nc.vector.quantize_mx(
-                out=codes[:, first : first + slots].bitcast(FP8X4),
-                scales=planes[:, first : first + slots],
-                in_=grouped[:, 4 * first : 4 * (first + slots)],
-            )
+        def quantize(grouped, codes, planes):
+            nc.vector.quantize_mx(out=codes.bitcast(FP8X4), scales=planes, in_=grouped)
 
         def multiply(codes, planes, g, e):
             cols = slice(e * C, (e + 1) * C)
@@ -110,23 +115,29 @@ def tile_routed_moe_kernel(tc, xT, w_words, w_scales, gate, offs, out):
                 stop=(g == PASSES - 1),
             )
 
-        grouped = []
+        rows = [[keep.tile([P, 2, HALF], U32, name="rows%d%d" % (g, h)) for h in range(HALVES)] for g in range(PASSES)]
         for g in range(PASSES):
-            pairs = [cast(g, u) for u in range(2)]
-            rows = [keep.tile([P, 2, HALF], U32, name="rows%d%d" % (g, h)) for h in range(HALVES)]
             for u in range(2):
+                pairs = cast(g, u)
                 for h in range(HALVES):
-                    gather(pairs[u], rows[h], u, h)
-            grouped.append(keep.tile([P, 4 * E * C], BF16, name="grouped%d" % g, align_bytes=64))
+                    gather(pairs, rows[g][h], u, h)
+        grouped = {}
+        for g in range(PASSES):
             for h in range(HALVES):
-                interleave(rows[h], grouped[g], h)
+                name, halves, place = GROUPED[g, h]
+                if place == 0:
+                    whole = keep.tile([P, halves, 4 * HALF], BF16, name=name, tag=name, align_bytes=64)
+                grouped[g, h] = whole[:, place, :]
+                interleave(rows[g][h], grouped[g, h])
 
         codes = keep.tile([P, PASSES, E * C], U32, name="codes", tag="late", align_bytes=64)
         planes = keep.tile([P, PASSES, E * C], U8, name="planes", align_bytes=64)
-        for g, first, slots in QUANTISERS:
-            quantize(grouped[g], codes[:, g, :], planes[:, g, :], first, slots)
-            for e in range(first // C, (first + slots) // C):
-                multiply(codes[:, g, :], planes[:, g, :], g, e)
+        for h in range(HALVES):
+            for g in range(PASSES):
+                cols = slice(h * HALF, (h + 1) * HALF)
+                quantize(grouped[g, h], codes[:, g, cols], planes[:, g, cols])
+                for i in range(HALF // C):
+                    multiply(codes[:, g, :], planes[:, g, :], g, h * (HALF // C) + i)
 
         for h in range(HALVES):
             for i in range(HALF // C):

@@ -22,16 +22,16 @@ LIST_COLS = HALF // 16
 FLOPS = 2 * K * N * E * C
 
 SHARES = {
-    0: ((0, 384, 176, 768), (768, 256, 0, 1024)),
+    0: ((0, 512, 0, 768), (768, 256, 0, 1024)),
     1: ((0, 0, 240, 512), (512, 0, 240, 1024)),
-    2: ((0, 0, 480, 1024),),
-    3: ((0, 0, 544, 1024),),
+    2: ((0, 0, 240, 512), (512, 0, 240, 1024)),
+    3: ((0, 0, 512, 1024),),
+    4: ((0, 0, 600, 1024),),
 }
 LATER = ((0, 0, 640, 1024),)
-LENDERS = {(1, 1): "grouped00", (2, 0): "grouped01", (2, 1): "grouped10", (3, 0): "grouped11", (3, 1): "grouped2"}
-GROUPED = {
-    (0, 0): ("grouped00", 1, 0), (0, 1): ("grouped01", 1, 0), (1, 0): ("grouped10", 1, 0), (1, 1): ("grouped11", 1, 0),
-    (2, 0): ("grouped2", 2, 0), (2, 1): ("grouped2", 2, 1), (3, 0): ("grouped3", 2, 0), (3, 1): ("grouped3", 2, 1),
+LENDERS = {
+    (1, 0, 1): "grouped00", (1, 1, 0): "grouped01", (2, 0, 0): "grouped10",
+    (2, 1, 0): "grouped11", (3, 0, 0): "grouped20", (3, 1, 0): "grouped21",
 }
 
 
@@ -50,7 +50,7 @@ def tile_routed_moe_kernel(tc, xT, w_words, w_scales, gate, offs, out):
             for u in range(2):
                 for part, (first, on_vector, on_gpsimd, last) in enumerate(SHARES.get(2 * g + u, LATER)):
                     name = "raw%d%d%d" % (g, u, part)
-                    raw[g, u, part] = keep.tile([P, 2, last - first], F32, name=name, tag=LENDERS.get((g, u), name), align_bytes=64)
+                    raw[g, u, part] = keep.tile([P, 2, last - first], F32, name=name, tag=LENDERS.get((g, u, part), name), align_bytes=64)
                     nc.sync.dma_start(raw[g, u, part][:], x_view[g, u][:, :, first:last])
                     if (g, u, part) == (0, 0, 0):
                         nc.sync.dma_start(offsets[:], offs)
@@ -124,10 +124,9 @@ def tile_routed_moe_kernel(tc, xT, w_words, w_scales, gate, offs, out):
         grouped = {}
         for g in range(PASSES):
             for h in range(HALVES):
-                name, halves, place = GROUPED[g, h]
-                if place == 0:
-                    whole = keep.tile([P, halves, 4 * HALF], BF16, name=name, tag=name, align_bytes=64)
-                grouped[g, h] = whole[:, place, :]
+                name = "grouped%d%d" % (g, h)
+                words = keep.tile([P, 4 * HALF], BF16, name=name, tag=name, align_bytes=64)
+                grouped[g, h] = words[:]
                 interleave(rows[g][h], grouped[g, h])
 
         codes = keep.tile([P, PASSES, E * C], U32, name="codes", tag="late", align_bytes=64)

@@ -22,15 +22,15 @@ LIST_COLS = HALF // 16
 FLOPS = 2 * K * N * E * C
 
 SHARES = {
-    0: ((0, 512, 0, 768), (768, 256, 0, 1024)),
-    1: ((0, 0, 240, 512), (512, 0, 240, 1024)),
-    2: ((0, 0, 240, 512), (512, 0, 240, 1024)),
+    0: ((0, 640, 0, 1024),),
+    1: ((0, 0, 496, 1024),),
+    2: ((0, 0, 496, 1024),),
     3: ((0, 0, 512, 1024),),
     4: ((0, 0, 600, 1024),),
 }
 LATER = ((0, 0, 640, 1024),)
 LENDERS = {
-    (1, 0, 1): "grouped00", (1, 1, 0): "grouped01", (2, 0, 0): "grouped10",
+    (1, 0, 0): "grouped00", (1, 1, 0): "grouped01", (2, 0, 0): "grouped10",
     (2, 1, 0): "grouped11", (3, 0, 0): "grouped20", (3, 1, 0): "grouped21",
 }
 

@@ -23,12 +23,12 @@ FLOPS = 2 * K * N * E * C
 
 SHARES = {
     0: ((0, 640, 0, 1024),),
-    1: ((0, 0, 496, 1024),),
-    2: ((0, 0, 496, 1024),),
-    3: ((0, 0, 512, 1024),),
-    4: ((0, 0, 600, 1024),),
+    1: ((0, 0, 528, 1024),),
+    2: ((0, 0, 528, 1024),),
+    3: ((0, 0, 560, 1024),),
+    4: ((0, 0, 640, 1024),),
 }
-LATER = ((0, 0, 640, 1024),)
+LATER = ((0, 0, 704, 1024),)
 LENDERS = {
     (1, 0, 0): "grouped00", (1, 1, 0): "grouped01", (2, 0, 0): "grouped10",
     (2, 1, 0): "grouped11", (3, 0, 0): "grouped20", (3, 1, 0): "grouped21",

@@ -45,6 +45,7 @@ def tile_routed_moe_kernel(tc, xT, w_words, w_scales, gate, offs, out):
         offsets = lists.tile([P, E * C // 16], U16, name="offsets")
 
         x_view = xT.rearrange("(g p u j) n -> g u p j n", p=P, u=2, j=2)
+        gate_sb = keep.tile([P, E * C], F32, name="gate_sb")
         raw = {}
         for g in range(PASSES):
             for u in range(2):
@@ -54,6 +55,8 @@ def tile_routed_moe_kernel(tc, xT, w_words, w_scales, gate, offs, out):
                     nc.sync.dma_start(raw[g, u, part][:], x_view[g, u][:, :, first:last])
                     if (g, u, part) == (0, 0, 0):
                         nc.sync.dma_start(offsets[:], offs)
+                    if (g, u, part) == (3, 0, 0):
+                        nc.sync.dma_start(gate_sb[:], gate)
 
         w_codes = keep.tile([P, E * PASSES, N], I32, name="w_codes", align_bytes=64)
         nc.sync.dma_start(w_codes[:], w_words.bitcast(I32).rearrange("e a p n o -> p (e a) (n o)"))
@@ -64,9 +67,6 @@ def tile_routed_moe_kernel(tc, xT, w_words, w_scales, gate, offs, out):
         scales_i32 = w_scales.bitcast(I32).rearrange("e a (q r) n -> r q (e a) n", r=4)
         for r in range(4):
             nc.sync.dma_start(planes_i32[r:P:32, :, :], scales_i32[r])
-
-        gate_sb = keep.tile([P, E * C], F32, name="gate_sb")
-        nc.sync.dma_start(gate_sb[:], gate)
 
         acc = [psum.tile([P, C], F32, name="acc%d" % e) for e in range(E)]
         sums = [keep.tile([P, HALF], F32, name="sums%d" % h) for h in range(HALVES)]

from contextlib import ExitStack

import concourse.mybir as mybir

F32 = mybir.dt.float32
BF16 = mybir.dt.bfloat16
U32 = mybir.dt.uint32
I32 = mybir.dt.int32
U16 = mybir.dt.uint16
U8 = mybir.dt.uint8
FP8X4 = mybir.dt.float8_e4m3fn_x4
MULT = mybir.AluOpType.mult
ADD = mybir.AluOpType.add

K, T, E, C, N = 2048, 1024, 4, 256, 128
P = 128
PASSES = K // 512
HALF = 512
HALVES = E * C // HALF
LIST_COLS = HALF // 16

FLOPS = 2 * K * N * E * C

SHARES = {
    0: ((0, 640, 0, 1024),),
    1: ((0, 0, 528, 1024),),
    2: ((0, 0, 528, 1024),),
    3: ((0, 0, 560, 1024),),
    4: ((0, 0, 640, 1024),),
}
LATER = ((0, 0, 704, 1024),)
LENDERS = {
    (1, 0, 0): "grouped00", (1, 1, 0): "grouped01", (2, 0, 0): "grouped10",
    (2, 1, 0): "grouped11", (3, 0, 0): "grouped20", (3, 1, 0): "grouped21",
}


def tile_routed_moe_kernel(tc, xT, w_words, w_scales, gate, offs, out):
    nc = tc.nc
    with ExitStack() as ctx:
        lists = ctx.enter_context(tc.tile_pool(name="lists", bufs=1))
        keep = ctx.enter_context(tc.tile_pool(name="keep", bufs=1))
        psum = ctx.enter_context(tc.psum_pool(name="psum", bufs=1))

        offsets = lists.tile([P, E * C // 16], U16, name="offsets")

        x_view = xT.rearrange("(g p u j) n -> g u p j n", p=P, u=2, j=2)
        gate_sb = keep.tile([P, E * C], F32, name="gate_sb")
        raw = {}
        for g in range(PASSES):
            for u in range(2):
                for part, (first, on_vector, on_gpsimd, last) in enumerate(SHARES.get(2 * g + u, LATER)):
                    name = "raw%d%d%d" % (g, u, part)
                    raw[g, u, part] = keep.tile([P, 2, last - first], F32, name=name, tag=LENDERS.get((g, u, part), name), align_bytes=64)
                    nc.sync.dma_start(raw[g, u, part][:], x_view[g, u][:, :, first:last])
                    if (g, u, part) == (0, 0, 0):
                        nc.sync.dma_start(offsets[:], offs)
                    if (g, u, part) == (3, 0, 0):
                        nc.sync.dma_start(gate_sb[:], gate)

        w_codes = keep.tile([P, E * PASSES, N], I32, name="w_codes", align_bytes=64)
        nc.sync.dma_start(w_codes[:], w_words.bitcast(I32).rearrange("e a p n o -> p (e a) (n o)"))

        w_planes = keep.tile([P, E * PASSES, N], U8, name="w_planes", align_bytes=64)
        nc.vector.memset(w_planes[:].rearrange("p s n -> p (s n)").bitcast(I32), 0)
        planes_i32 = w_planes[:].bitcast(I32)
        scales_i32 = w_scales.bitcast(I32).rearrange("e a (q r) n -> r q (e a) n", r=4)
        for r in range(4):
            nc.sync.dma_start(planes_i32[r:P:32, :, :], scales_i32[r])

        acc = [psum.tile([P, C], F32, name="acc%d" % e) for e in range(E)]
        sums = [keep.tile([P, HALF], F32, name="sums%d" % h) for h in range(HALVES)]
        result = keep.tile([P, T], F32, name="result")

        def cast(g, u):
            last_pair = (g, u) == (PASSES - 1, 1)
            pairs = keep.tile([P, 2 * T], BF16, name="pairs%d%d" % (g, u), tag="late" if last_pair else "pairs%d%d" % (g, u), align_bytes=64)
            dst = pairs[:].rearrange("p (n j) -> p n j", j=2)
            for part, (first, on_vector, on_gpsimd, last) in enumerate(SHARES.get(2 * g + u, LATER)):
                src = raw[g, u, part][:].rearrange("p j n -> p n j")
                cut = on_vector
                mid = on_vector + on_gpsimd
                if cut:
                    nc.vector.tensor_copy(out=dst[:, first : first + cut, :], in_=src[:, 0:cut, :])
                if on_gpsimd:
                    nc.gpsimd.tensor_scalar(
                        out=dst[:, first + cut : first + mid, :], in0=src[:, cut:mid, :], scalar1=1.0, scalar2=0.0, op0=MULT, op1=ADD
                    )
                if first + mid < last:
                    nc.scalar.copy(out=dst[:, first + mid : last, :], in_=src[:, mid : last - first, :])
            return pairs

        def gather(pairs, rows, u, h):
            window = pairs[:].bitcast(U32)
            nc.vector.tensor_copy(rows[:, u, :], window.indirect(offsets[:, h * LIST_COLS : (h + 1) * LIST_COLS]))

        def interleave(rows, grouped):
            nc.scalar.copy(
                out=grouped.bitcast(U32).rearrange("p (c u) -> p c u", u=2),
                in_=rows[:].rearrange("p u c -> p c u"),
            )

        def quantize(grouped, codes, planes):
            nc.vector.quantize_mx(out=codes.bitcast(FP8X4), scales=planes, in_=grouped)

        def multiply(codes, planes, g, e):
            cols = slice(e * C, (e + 1) * C)
            nc.tensor.matmul_mx(
                out=acc[e][:],
                lhsT=w_codes[:, e * PASSES + g, :].bitcast(FP8X4),
                lhsT_scale=w_planes[:, e * PASSES + g, :],
                rhs=codes[:, cols].bitcast(FP8X4),
                rhs_scale=planes[:, cols],
                start=(g == 0),
                stop=(g == PASSES - 1),
            )

        rows = [[keep.tile([P, 2, HALF], U32, name="rows%d%d" % (g, h)) for h in range(HALVES)] for g in range(PASSES)]
        for g in range(PASSES):
            for u in range(2):
                pairs = cast(g, u)
                for h in range(HALVES):
                    gather(pairs, rows[g][h], u, h)
        grouped = {}
        for g in range(PASSES):
            for h in range(HALVES):
                name = "grouped%d%d" % (g, h)
                words = keep.tile([P, 4 * HALF], BF16, name=name, tag=name, align_bytes=64)
                grouped[g, h] = words[:]
                interleave(rows[g][h], grouped[g, h])

        codes = keep.tile([P, PASSES, E * C], U32, name="codes", tag="late", align_bytes=64)
        planes = keep.tile([P, PASSES, E * C], U8, name="planes", align_bytes=64)
        for h in range(HALVES):
            for g in range(PASSES):
                cols = slice(h * HALF, (h + 1) * HALF)
                quantize(grouped[g, h], codes[:, g, cols], planes[:, g, cols])
                for i in range(HALF // C):
                    multiply(codes[:, g, :], planes[:, g, :], g, h * (HALF // C) + i)

        for h in range(HALVES):
            for i in range(HALF // C):
                nc.scalar.copy(out=sums[h][:, i * C : (i + 1) * C], in_=acc[h * (HALF // C) + i][:])
            nc.vector.tensor_tensor(
                out=result[:].indirect(offsets[:, h * LIST_COLS : (h + 1) * LIST_COLS]),
                in0=sums[h][:],
                in1=gate_sb[:, h * HALF : (h + 1) * HALF],
                op=MULT,
            )
        nc.sync.dma_start(out, result[:])
